import numpy as np, ml_dtypes
CORES = [33,34,161,162,289,290,417,418]
N = 8
TK = 128
COEF = [[3,1,1,1,1,1,1,1],[1,3,1,1,1,1,1,1],[1,1,3,1,1,1,1,1],[1,1,1,3,1,1,1,1],[1,1,1,1,3,1,1,1],[1,1,1,1,1,3,1,1],[1,1,1,1,1,1,3,1],[1,1,1,1,1,1,1,3]]
def setup_inputs(rng):
    return {"x": rng.standard_normal((N, 128, TK), dtype=np.float32).astype(ml_dtypes.bfloat16), "a": (rng.standard_normal((N, 128, 128), dtype=np.float32) / 11).astype(ml_dtypes.bfloat16)}
def setup_inputs_big(rng):
    d = setup_inputs(rng)
    for k in ("x", "a"): d[k] = (d[k].astype(np.float32) * 1024.0).astype(d[k].dtype)
    return d
def setup_inputs_small(rng):
    d = setup_inputs(rng)
    for k in ("x", "a"): d[k] = (d[k].astype(np.float32) * (1 / 1024.0)).astype(d[k].dtype)
    return d
def setup_inputs_apart(rng):
    d = setup_inputs(rng)
    f = (10.0 ** rng.permutation(np.linspace(-1.5, 1.5, N))).astype(np.float32).reshape(N, 1, 1)
    for k in ("x", "a"): d[k] = (d[k].astype(np.float32) * f).astype(d[k].dtype)
    return d
def reference(x, a):
    X, A = x.astype(np.float64), a.astype(np.float64)
    y = np.stack([A[r].T @ sum(COEF[r][j] * X[j] for j in range(N)) for r in range(N)])
    return {"y": y.astype(ml_dtypes.bfloat16)}

@@ -1,0 +1,91 @@
+from concourse.bass import DstId, RemoteDMATransfer
+
+P, W = 128, 128
+SCRATCH = {
+    "xd": ("dram", [P, W], "bfloat16"),
+    "ld": ("dram", [3, P, W], "bfloat16"),
+    "xs": ("sbuf", [P, W], "bfloat16"),
+    "am": ("sbuf", [P, W], "bfloat16"),
+    "qa": ("sbuf", [P, W], "bfloat16"),
+    "qb": ("sbuf", [P, W], "bfloat16"),
+    "ys": ("sbuf", [P, W], "bfloat16"),
+    "ps": ("psum", [P, W], "float32"),
+}
+SEMAPHORES = ["lx", "lm", "arr1", "arr2", "sent", "mm", "cp", "st"]
+
+
+def _peers(c, T, topo):
+    ranks = sorted(T.cores)
+    home = [k for k in ranks if (topo.host(k), topo.chip(k)) == (topo.host(c), topo.chip(c))]
+    far = [k for k in ranks if topo.rack(topo.host(k)) != topo.rack(topo.host(c)) and topo.may_write(c, k)]
+    near = [k for k in ranks if topo.same_plane(c, k) and topo.may_write(c, k)]
+    return home, far, near
+
+
+def _mask(core, dsts, topo):
+    m = topo.mask(core, dsts[0])
+    for d in dsts[1:]:
+        m &= topo.mask(core, d)
+    return m
+
+
+def _ids(core, dsts, topo):
+    out = []
+    for d in dsts:
+        rid, pid = topo.addr(d, core)
+        out.append(DstId(rid=rid, pnc=pid))
+    return out
+
+
+def rank_program(g, core, T, topo):
+    rank = T.rank_of(core)
+    if rank is None:
+        return
+    S = T.sem
+    coef = T.tables["COEF"]
+    n = len(T.cores)
+    if any(coef[r][j] != 1 for r in range(n) for j in range(n) if r != j) or coef[rank][rank] < 1:
+        raise ValueError("this kernel is built for COEF = 1 off the diagonal")
+    extra = coef[rank][rank] - 1
+
+    home, far, near = _peers(core, T, topo)
+    if (len(home), len(far), len(near)) != (2, 2, 2):
+        raise ValueError("this kernel is built for two ranks a chip on a ring of four hosts")
+    k = home.index(core)
+    partner, peer = home[1 - k], near[k]
+
+    g.sync.dma_start(T.xd[:, :], T.x[:, :]).then_inc(S.lx, 16)
+    g.sync.dma_start(T.am[:, :], T.a[:, :]).then_inc(S.lm, 16)
+    g.sync.dma_start(T.xs[:, :], T.x[:, :]).then_inc(S.lm, 16)
+
+    d1 = far + [partner]
+    slot = [1 + _peers(d, T, topo)[1].index(core) for d in far] + [0]
+    m1 = _mask(core, d1, topo)
+    e1 = bin(m1).count("1")
+    g.wait_ge(S.lx, 16)
+    g.remote_dma_fused([RemoteDMATransfer(dst_ids=_ids(core, d1, topo), dma_engine_mask=m1, remote_sem=S.arr1,
+                                          srcs=[T.xd[:, :]], dsts=[T.ld[s] for s in slot], alu_op=0)],
+                       local_sem=S.sent)
+
+    d2 = [peer, partner]
+    m2 = _mask(core, d2, topo)
+    e2 = bin(m2).count("1")
+    g.wait_ge(S.arr1, 3 * e1)
+    g.remote_dma_fused([RemoteDMATransfer(dst_ids=_ids(core, d2, topo), dma_engine_mask=m2, remote_sem=S.arr2,
+                                          srcs=[T.xd[:, :], T.ld[0], T.ld[1], T.ld[2]],
+                                          dsts=[T.qb[:, :], T.qa[:, :]], alu_op=1)],
+                       local_sem=S.sent)
+    g.wait_ge(S.sent, e1 + e2)
+
+    terms = [T.xs] * extra + [T.qa, T.qb]
+    g.tensor.wait_ge(S.lm, 32)
+    for i, t in enumerate(terms):
+        if i == extra:
+            g.tensor.wait_ge(S.arr2, 2 * e2)
+        mm = g.tensor.matmul(T.ps[:, :], T.am[:, :], t[:, :], i == 0, i == len(terms) - 1)
+    mm.then_inc(S.mm, 1)
+    g.vector.wait_ge(S.mm, 1)
+    g.vector.tensor_copy(T.ys[:, :], T.ps[:, :]).then_inc(S.cp, 1)
+    g.sync.wait_ge(S.cp, 1)
+    g.sync.dma_start(T.y[:, :], T.ys[:, :]).then_inc(S.st, 16)
+    g.sync.wait_ge(S.st, 16)

@@ -11,7 +11,7 @@ SCRATCH = {
     "ys": ("sbuf", [P, W], "bfloat16"),
     "ps": ("psum", [P, W], "float32"),
 }
-SEMAPHORES = ["lx", "lm", "arr1", "arr2", "sent", "mm", "cp", "st"]
+SEMAPHORES = ["lx", "lm", "arr1", "arra", "arrb", "sent", "mm", "cp", "st"]
 
 
 def _peers(c, T, topo):
@@ -27,6 +27,15 @@ def _mask(core, dsts, topo):
     for d in dsts[1:]:
         m &= topo.mask(core, d)
     return m
+
+
+def _bits(m):
+    return [1 << i for i in range(m.bit_length()) if (m >> i) & 1]
+
+
+def _slot(src, dst, T, topo):
+    near = _peers(dst, T, topo)[2]
+    return 1 + near.index(src) if src in near else 0
 
 
 def _ids(core, dsts, topo):
@@ -52,36 +61,35 @@ def rank_program(g, core, T, topo):
     if (len(home), len(far), len(near)) != (2, 2, 2):
         raise ValueError("this kernel is built for two ranks a chip on a ring of four hosts")
     k = home.index(core)
-    partner, peer = home[1 - k], near[k]
+    partner, peer = home[1 - k], far[k]
 
     g.sync.dma_start(T.xd[:, :], T.x[:, :]).then_inc(S.lx, 16)
     g.sync.dma_start(T.am[:, :], T.a[:, :]).then_inc(S.lm, 16)
     g.sync.dma_start(T.xs[:, :], T.x[:, :]).then_inc(S.lm, 16)
 
-    d1 = far + [partner]
-    slot = [1 + _peers(d, T, topo)[1].index(core) for d in far] + [0]
-    m1 = _mask(core, d1, topo)
-    e1 = bin(m1).count("1")
+    off = _bits(_mask(core, near + [peer], topo))
+    own = [b for b in _bits(topo.mask(core, partner)) if b not in off]
+    h = len(off) // 2
+
     g.wait_ge(S.lx, 16)
-    g.remote_dma_fused([RemoteDMATransfer(dst_ids=_ids(core, d1, topo), dma_engine_mask=m1, remote_sem=S.arr1,
-                                          srcs=[T.xd[:, :]], dsts=[T.ld[s] for s in slot], alu_op=0)],
-                       local_sem=S.sent)
+    w1 = [(near[0], off[:h]), (near[1], off[h:]), (partner, own)]
+    g.remote_dma_fused([RemoteDMATransfer(dst_ids=_ids(core, [d], topo), dma_engine_mask=sum(e), remote_sem=S.arr1,
+                                          src=T.xd[:, :], dst=T.ld[_slot(core, d, T, topo)], alu_op=0)
+                        for d, e in w1], local_sem=S.sent)
 
-    d2 = [peer, partner]
-    m2 = _mask(core, d2, topo)
-    e2 = bin(m2).count("1")
-    g.wait_ge(S.arr1, 3 * e1)
-    g.remote_dma_fused([RemoteDMATransfer(dst_ids=_ids(core, d2, topo), dma_engine_mask=m2, remote_sem=S.arr2,
-                                          srcs=[T.xd[:, :], T.ld[0], T.ld[1], T.ld[2]],
-                                          dsts=[T.qb[:, :], T.qa[:, :]], alu_op=1)],
-                       local_sem=S.sent)
-    g.wait_ge(S.sent, e1 + e2)
+    g.wait_ge(S.arr1, 2 * h + len(own))
+    four = [T.xd[:, :], T.ld[0], T.ld[1], T.ld[2]]
+    g.remote_dma_fused([RemoteDMATransfer(dst_ids=_ids(core, [peer], topo), dma_engine_mask=sum(off), remote_sem=S.arrb,
+                                          srcs=four, dsts=[T.qb[:, :]], alu_op=1),
+                        RemoteDMATransfer(dst_ids=_ids(core, [partner], topo), dma_engine_mask=sum(own), remote_sem=S.arra,
+                                          srcs=four, dsts=[T.qa[:, :]], alu_op=1)], local_sem=S.sent)
+    g.wait_ge(S.sent, 2 * (len(off) + len(own)))
 
-    terms = [T.xs] * extra + [T.qa, T.qb]
+    terms = [(T.xs, None, 0)] * extra + [(T.qa, S.arra, len(own)), (T.qb, S.arrb, len(off))]
     g.tensor.wait_ge(S.lm, 32)
-    for i, t in enumerate(terms):
-        if i == extra:
-            g.tensor.wait_ge(S.arr2, 2 * e2)
+    for i, (t, sem, cnt) in enumerate(terms):
+        if sem is not None:
+            g.tensor.wait_ge(sem, cnt)
         mm = g.tensor.matmul(T.ps[:, :], T.am[:, :], t[:, :], i == 0, i == len(terms) - 1)
     mm.then_inc(S.mm, 1)
     g.vector.wait_ge(S.mm, 1)

from concourse.bass import DstId, RemoteDMATransfer

P, W = 128, 128
SCRATCH = {
    "xd": ("dram", [P, W], "bfloat16"),
    "ld": ("dram", [3, P, W], "bfloat16"),
    "xs": ("sbuf", [P, W], "bfloat16"),
    "am": ("sbuf", [P, W], "bfloat16"),
    "qa": ("sbuf", [P, W], "bfloat16"),
    "qb": ("sbuf", [P, W], "bfloat16"),
    "ys": ("sbuf", [P, W], "bfloat16"),
    "ps": ("psum", [P, W], "float32"),
}
SEMAPHORES = ["lx", "lm", "arr1", "arra", "arrb", "sent", "mm", "cp", "st"]


def _peers(c, T, topo):
    ranks = sorted(T.cores)
    home = [k for k in ranks if (topo.host(k), topo.chip(k)) == (topo.host(c), topo.chip(c))]
    far = [k for k in ranks if topo.rack(topo.host(k)) != topo.rack(topo.host(c)) and topo.may_write(c, k)]
    near = [k for k in ranks if topo.same_plane(c, k) and topo.may_write(c, k)]
    return home, far, near


def _mask(core, dsts, topo):
    m = topo.mask(core, dsts[0])
    for d in dsts[1:]:
        m &= topo.mask(core, d)
    return m


def _bits(m):
    return [1 << i for i in range(m.bit_length()) if (m >> i) & 1]


def _slot(src, dst, T, topo):
    near = _peers(dst, T, topo)[2]
    return 1 + near.index(src) if src in near else 0


def _ids(core, dsts, topo):
    out = []
    for d in dsts:
        rid, pid = topo.addr(d, core)
        out.append(DstId(rid=rid, pnc=pid))
    return out


def rank_program(g, core, T, topo):
    rank = T.rank_of(core)
    if rank is None:
        return
    S = T.sem
    coef = T.tables["COEF"]
    n = len(T.cores)
    if any(coef[r][j] != 1 for r in range(n) for j in range(n) if r != j) or coef[rank][rank] < 1:
        raise ValueError("this kernel is built for COEF = 1 off the diagonal")
    extra = coef[rank][rank] - 1

    home, far, near = _peers(core, T, topo)
    if (len(home), len(far), len(near)) != (2, 2, 2):
        raise ValueError("this kernel is built for two ranks a chip on a ring of four hosts")
    k = home.index(core)
    partner, peer = home[1 - k], far[k]

    g.sync.dma_start(T.xd[:, :], T.x[:, :]).then_inc(S.lx, 16)
    g.sync.dma_start(T.am[:, :], T.a[:, :]).then_inc(S.lm, 16)
    g.sync.dma_start(T.xs[:, :], T.x[:, :]).then_inc(S.lm, 16)

    off = _bits(_mask(core, near + [peer], topo))
    own = [b for b in _bits(topo.mask(core, partner)) if b not in off]
    h = len(off) // 2

    g.wait_ge(S.lx, 16)
    w1 = [(near[0], off[:h]), (near[1], off[h:]), (partner, own)]
    g.remote_dma_fused([RemoteDMATransfer(dst_ids=_ids(core, [d], topo), dma_engine_mask=sum(e), remote_sem=S.arr1,
                                          src=T.xd[:, :], dst=T.ld[_slot(core, d, T, topo)], alu_op=0)
                        for d, e in w1], local_sem=S.sent)

    g.wait_ge(S.arr1, 2 * h + len(own))
    four = [T.xd[:, :], T.ld[0], T.ld[1], T.ld[2]]
    g.remote_dma_fused([RemoteDMATransfer(dst_ids=_ids(core, [peer], topo), dma_engine_mask=sum(off), remote_sem=S.arrb,
                                          srcs=four, dsts=[T.qb[:, :]], alu_op=1),
                        RemoteDMATransfer(dst_ids=_ids(core, [partner], topo), dma_engine_mask=sum(own), remote_sem=S.arra,
                                          srcs=four, dsts=[T.qa[:, :]], alu_op=1)], local_sem=S.sent)
    g.wait_ge(S.sent, 2 * (len(off) + len(own)))

    terms = [(T.xs, None, 0)] * extra + [(T.qa, S.arra, len(own)), (T.qb, S.arrb, len(off))]
    g.tensor.wait_ge(S.lm, 32)
    for i, (t, sem, cnt) in enumerate(terms):
        if sem is not None:
            g.tensor.wait_ge(sem, cnt)
        mm = g.tensor.matmul(T.ps[:, :], T.am[:, :], t[:, :], i == 0, i == len(terms) - 1)
    mm.then_inc(S.mm, 1)
    g.vector.wait_ge(S.mm, 1)
    g.vector.tensor_copy(T.ys[:, :], T.ps[:, :]).then_inc(S.cp, 1)
    g.sync.wait_ge(S.cp, 1)
    g.sync.dma_start(T.y[:, :], T.ys[:, :]).then_inc(S.st, 16)
    g.sync.wait_ge(S.st, 16)
